import numpy as np
import ml_dtypes


def mxq(x, axis, fmt="e4m3"):
    dtype, down = {"e4m3": (ml_dtypes.float8_e4m3fn, 7), "e5m2": (ml_dtypes.float8_e5m2, 14)}[fmt]
    v = np.moveaxis(np.asarray(x, np.float32).astype(ml_dtypes.bfloat16).astype(np.float64), axis, -1)
    blocks = v.reshape(v.shape[:-1] + (-1, 32))
    amax = np.abs(blocks).max(-1, keepdims=True)
    byte = np.maximum(np.where(amax > 0, np.frexp(amax)[1] - 1 + 127, 0) - down, 1)
    scale = np.exp2(byte - 127.0)
    codes = (blocks / scale).astype(np.float32).astype(dtype).astype(np.float64)
    return np.moveaxis((codes * scale).reshape(v.shape), -1, axis)


WIDE = False


def mx_kscale(k):
    if not WIDE:
        return np.ones(k)
    levels = np.array([10, -10, 5, -5, 0])
    if k % 512:
        return np.exp2(np.random.permutation(np.resize(levels, k // 32))).repeat(32)
    a = np.empty((k // 512, 16))
    for p in range(k // 512):
        a[p, :8] = np.random.permutation(np.resize(levels, 8))
        for g in range(8):
            far = levels[np.abs(levels - a[p, g]) >= 10]
            a[p, g + 8] = far[np.random.randint(len(far))]
    return np.exp2(a.ravel()).repeat(32)


def f64(x):
    return np.asarray(x).astype(np.float64)


def striped(idx):
    return np.tile(idx.reshape(-1, 16).T, (8, 1)).astype(np.uint16)


def unstriped(offs):
    return offs[:16].T.reshape(-1).astype(np.int64)


def striped8(idx):
    return np.concatenate([x.reshape(-1, 16).T for x in idx]).astype(np.uint16)


def runs(offs, k):
    lists = np.stack([offs[16 * r : 16 * r + 16].T.reshape(-1) for r in range(8)]).astype(np.int64)
    return lists[np.arange(k) % 512 // 64]


def pack_weight(w):
    k, n = w.shape
    w = f64(np.asarray(w, np.float32).astype(ml_dtypes.bfloat16)).reshape(k // 32, 32, n)
    amax = np.abs(w).max(1)
    byte = np.clip(np.where(amax > 0, np.frexp(amax)[1] - 1 + 127 - 7, 1), 1, 254)
    scaled = (w * np.exp2(127.0 - byte)[:, None, :]).reshape(k, n).astype(np.float32)
    words = np.ascontiguousarray(scaled.reshape(k // 512, 128, 4, n).transpose(0, 1, 3, 2)).astype(ml_dtypes.float8_e4m3fn).view(np.uint8)
    return words, np.ascontiguousarray(byte.astype(np.uint8).reshape(k // 512, 16, n))


def unpack_weight(words, scales):
    g, p, n, _ = words.shape
    vals = np.ascontiguousarray(words).view(ml_dtypes.float8_e4m3fn).astype(np.float64) * np.repeat(np.exp2(scales.astype(np.float64) - 127.0), 8, axis=1)[..., None]
    return vals.transpose(0, 1, 3, 2).reshape(g * 512, n)


E2M1 = np.array([0.0, 0.5, 1.0, 1.5, 2.0, 3.0, 4.0, 6.0, -0.0, -0.5, -1.0, -1.5, -2.0, -3.0, -4.0, -6.0])


def pack_fp4(w):
    k, n = w.shape
    w = f64(np.asarray(w, np.float32).astype(ml_dtypes.bfloat16)).reshape(k // 32, 32, n)
    amax = np.abs(w).max(1)
    mant, ex = np.frexp(amax / 6.0)
    byte = np.clip(np.where(amax > 0, np.where(mant > 0.5, ex, ex - 1) + 127, 1), 1, 254)
    scaled = (w * np.exp2(127.0 - byte)[:, None, :]).reshape(k, n).astype(np.float32)
    c = np.ascontiguousarray(scaled.reshape(k // 512, 128, 4, n).transpose(0, 1, 3, 2)).astype(ml_dtypes.float4_e2m1fn).view(np.uint8) & 0xF
    words = (c[..., 0::2] | (c[..., 1::2] << 4)).reshape(k // 512, 128, 2 * n)
    return np.ascontiguousarray(words), np.ascontiguousarray(byte.astype(np.uint8).reshape(k // 512, 16, n))


def unpack_fp4(words, scales):
    g, _, n = scales.shape
    words = np.ascontiguousarray(words).reshape(g, 128, n, 2)
    nib = np.empty((g, 128, n, 4), np.uint8)
    nib[..., 0::2] = words & 0xF
    nib[..., 1::2] = words >> 4
    vals = E2M1[nib] * np.repeat(np.exp2(scales.astype(np.float64) - 127.0), 8, axis=1)[..., None]
    return vals.transpose(0, 1, 3, 2).reshape(g * 512, n)


K, T, S, H, W, G = 512, 1024, 512, 512, 256, 2048


def setup_inputs():
    n = np.random.standard_normal
    s = mx_kscale(K)[:, None]
    packed_xT = pack_weight(n((K, T)) * s)
    packed_w1 = pack_fp4(n((K, H)) / np.sqrt(2 * K) / s)
    packed_w2 = pack_fp4(n((K, H)) / np.sqrt(2 * K) / s)
    packed_dT = pack_weight(n((K, G)) / s)
    perm = np.stack([np.random.permutation(S) for _ in range(8)])
    return {
        "x_words": packed_xT[0],
        "x_scales": packed_xT[1],
        "w1_words": packed_w1[0],
        "w1_scales": packed_w1[1],
        "w2_words": packed_w2[0],
        "w2_scales": packed_w2[1],
        "gs": (np.random.uniform(0.5, 1.5, (K, 1)) * s).astype(np.float32),
        "d_words": packed_dT[0],
        "d_scales": packed_dT[1],
        "offs": striped(np.random.permutation(T)[:S]),
        "hz": striped8(np.random.randint(0, T, (8, S))),
        "n1": striped8(perm[:, :W]),
        "n2": striped8(perm[:, W:]),
        "k1": striped8(np.random.randint(0, G, (8, H))),
        "n3": striped8(np.stack([np.random.permutation(S) for _ in range(8)])),
        "n4": striped8(np.stack([np.random.permutation(S) for _ in range(8)])),
    }


def reference(x_words, x_scales, w1_words, w1_scales, w2_words, w2_scales, gs, d_words, d_scales, offs, hz, n1, n2, k1, n3, n4):
    d_k1 = unpack_weight(d_words, d_scales)[np.arange(K)[:, None], runs(k1, K)]
    xq = unpack_weight(x_words, x_scales)[:, unstriped(offs)]
    x_hz = unpack_weight(x_words, x_scales)[np.arange(K)[:, None], runs(hz, K)]
    y = unpack_fp4(w1_words, w1_scales).T @ xq + unpack_fp4(w2_words, w2_scales).T @ x_hz
    pa = y[np.arange(H)[:, None], runs(n1, H)]
    pb = y[np.arange(H)[:, None], runs(n2, H)]
    rb = np.maximum(pa, pb)
    ra = pa / (np.abs(pb) + 0.5)
    ds = np.zeros((H, S))
    ds[np.arange(H)[:, None], runs(n1, H)] = ra
    dt = ds.copy()
    dt[np.arange(H)[:, None], runs(n2, H)] = rb
    z = f64(gs) * dt
    h = 0.0625 * ((d_k1.T @ mxq(z, 0, "e4m3")))
    ds2 = np.zeros((H, S))
    ds2[np.arange(H)[:, None], runs(n3, H)] = h
    return np.maximum(h, ds2[np.arange(H)[:, None], runs(n4, H)])

@@ -1,0 +1,200 @@
+from contextlib import ExitStack
+
+import concourse.mybir as mybir
+
+F32 = mybir.dt.float32
+BF16 = mybir.dt.bfloat16
+I32 = mybir.dt.int32
+U32 = mybir.dt.uint32
+U16 = mybir.dt.uint16
+U8 = mybir.dt.uint8
+FP8X4 = mybir.dt.float8_e4m3fn_x4
+FP4X4 = mybir.dt.float4_e2m1fn_x4
+ACT = mybir.ActivationFunctionType
+ALU = mybir.AluOpType
+
+P = 128
+K, T, S, H, W, G = 512, 1024, 512, 512, 256, 2048
+NT = 4
+FLOPS = 3 * 2 * K * H * S
+
+
+def tile_picked_thqratiorelay_none_p_kernel(
+    tc, x_words, x_scales, w1_words, w1_scales, w2_words, w2_scales, gs, d_words, d_scales,
+    offs, hz, n1, n2, k1, n3, n4, out,
+):
+    nc = tc.nc
+    with ExitStack() as ctx:
+        keep = ctx.enter_context(tc.tile_pool(name="keep", bufs=1))
+        psum = ctx.enter_context(tc.psum_pool(name="psum", bufs=1))
+
+        def sb(name, shape, dtype):
+            return keep.tile(shape, dtype, name=name, align_bytes=64)
+
+        def zeroed_bytes(name, width):
+            tile = sb(name, [P, width], U8)
+            nc.vector.memset(tile[:].bitcast(I32), 0)
+            return tile
+
+        def load_list(name, src):
+            tile = sb(name, list(src.shape), U16)
+            nc.sync.dma_start(tile[:], src)
+            return tile
+
+        def spread_rows(scales):
+            rows = scales[0].bitcast(I32)
+            return rows.unsqueeze(1).to_broadcast([16, 8, rows.shape[1]])
+
+        def place_rows(queue, plane, spread):
+            for j in range(4):
+                queue.dma_start(plane[j:P:32, :].bitcast(I32), spread[8 * j:P:32, :].bitcast(I32))
+
+        xs_tab = sb("xs_tab", [P, T], U8)
+        ws_raw = sb("ws_raw", [P, 2 * H], U8)
+        ww_raw = [sb("ww_raw%d" % i, [P, 2 * H], U8) for i in range(2)]
+        xw_tab = sb("xw_tab", [P, T], I32)
+        nc.scalar.dma_start(xs_tab[:].bitcast(I32), spread_rows(x_scales))
+        hz_t = load_list("hz_t", hz)
+        offs_t = load_list("offs_t", offs)
+        nc.scalar.dma_start(ws_raw[:, 0:H].bitcast(I32), spread_rows(w1_scales))
+        nc.scalar.dma_start(ws_raw[:, H:2 * H].bitcast(I32), spread_rows(w2_scales))
+        nc.sync.dma_start(xw_tab[:], x_words[0].rearrange("p n r -> p (n r)").bitcast(I32))
+        nc.gpsimd.dma_start(ww_raw[0][:].bitcast(I32), w1_words[0].bitcast(I32))
+        nc.gpsimd.dma_start(ww_raw[1][:].bitcast(I32), w2_words[0].bitcast(I32))
+
+        ds_tab = sb("ds_tab", [P, G], U8)
+        gs_t = sb("gs_t", [P, NT], F32)
+        nc.gpsimd.dma_start(ds_tab[:].bitcast(I32), spread_rows(d_scales))
+        nc.gpsimd.dma_start(gs_t[:], gs.rearrange("(p t) o -> p (t o)", t=NT))
+        k1_t = load_list("k1_t", k1)
+        dw_tab = sb("dw_tab", [P, G], I32)
+        nc.sync.dma_start(dw_tab[:], d_words[0].rearrange("p n r -> p (n r)").bitcast(I32))
+        n2_t = load_list("n2_t", n2)
+        n1_t = load_list("n1_t", n1)
+        n3_t = load_list("n3_t", n3)
+        n4_t = load_list("n4_t", n4)
+
+        ws_plane = zeroed_bytes("ws_plane", 2 * H)
+        xs_plane = zeroed_bytes("xs_plane", 2 * S)
+        ds_plane = zeroed_bytes("ds_plane", H)
+
+        ws_dealt = sb("ws_dealt", [P, 2 * H], U8)
+        nc.vector.tensor_copy(
+            ws_dealt[:].rearrange("p (i t m) -> p i t m", i=2, t=NT),
+            ws_raw[:].rearrange("p (i m t) -> p i t m", i=2, t=NT),
+        )
+        place_rows(nc.sync, ws_plane, ws_dealt)
+        ww = [sb("ww%d" % i, [P, 2 * H], U8) for i in range(2)]
+        for i in range(2):
+            nc.scalar.copy(
+                ww[i][:].bitcast(U16).rearrange("p (t m) -> p t m", t=NT),
+                ww_raw[i][:].bitcast(U16).rearrange("p (m t) -> p t m", t=NT),
+            )
+        gs_wide = [sb("gs_wide%d" % t, [P, W], F32) for t in range(NT)]
+        for t in range(NT):
+            nc.scalar.copy(gs_wide[t][:], gs_t[:, t:t + 1].to_broadcast([P, W]))
+
+        xs_got = sb("xs_got", [P, 2 * S], U8)
+        nc.vector.tensor_copy(xs_got[:, S:2 * S], xs_tab[:].indirect(hz_t[:]))
+        nc.vector.tensor_copy(xs_got[:, 0:S], xs_tab[:].indirect(offs_t[:]))
+        place_rows(nc.sync, xs_plane, xs_got)
+        xw_got = [sb("xw_got%d" % i, [P, S], U32) for i in range(2)]
+        nc.vector.tensor_copy(xw_got[0][:], xw_tab[:].bitcast(U32).indirect(offs_t[:]))
+        nc.vector.tensor_copy(xw_got[1][:], xw_tab[:].bitcast(U32).indirect(hz_t[:]))
+
+        y_bank = [psum.tile([P, S], F32, name="y_bank%d" % t, tag="bank%d" % t) for t in range(NT)]
+        for t in (1, 3, 0, 2):
+            for i in range(2):
+                nc.tensor.matmul_mx(
+                    out=y_bank[t][:],
+                    lhsT=ww[i][:, 2 * P * t:2 * P * (t + 1)].bitcast(FP4X4),
+                    lhsT_scale=ws_plane[:, H * i + P * t:H * i + P * (t + 1)],
+                    rhs=xw_got[i][:].bitcast(FP8X4),
+                    rhs_scale=xs_plane[:, S * i:S * (i + 1)],
+                    start=(i == 0),
+                    stop=(i == 1),
+                )
+
+        ds_got = sb("ds_got", [P, H], U8)
+        nc.vector.tensor_copy(ds_got[:], ds_tab[:].indirect(k1_t[:]))
+        ds_dealt = sb("ds_dealt", [P, H], U8)
+        nc.vector.tensor_copy(
+            ds_dealt[:].rearrange("p (t m) -> p t m", t=NT), ds_got[:].rearrange("p (m t) -> p t m", t=NT)
+        )
+        place_rows(nc.gpsimd, ds_plane, ds_dealt)
+        dw_got = sb("dw_got", [P, H], U32)
+        nc.vector.tensor_copy(dw_got[:], dw_tab[:].bitcast(U32).indirect(k1_t[:]))
+        dw = sb("dw", [P, H], U32)
+        nc.vector.tensor_copy(
+            dw[:].rearrange("p (t m) -> p t m", t=NT), dw_got[:].rearrange("p (m t) -> p t m", t=NT)
+        )
+
+        z_win = {}
+        for t in (1, 3, 0, 2):
+            y = sb("y%d" % t, [P, S], F32)
+            nc.scalar.copy(y[:], y_bank[t][:])
+            pa = sb("pa%d" % t, [P, W], F32)
+            pb = sb("pb%d" % t, [P, W], F32)
+            nc.scalar.activation(pb[:], y[:].indirect(n2_t[:]), ACT.Copy)
+            nc.scalar.activation(pa[:], y[:].indirect(n1_t[:]), ACT.Copy)
+            size = sb("size%d" % t, [P, W], F32)
+            root = keep.tile([P, W], F32, name="root%d" % t, tag="turn%d" % t, align_bytes=64)
+            inv = sb("inv%d" % t, [P, W], F32)
+            pag = sb("pag%d" % t, [P, W], F32)
+            big = sb("big%d" % t, [P, W], F32)
+            nc.scalar.activation(size[:], pb[:], ACT.Abs)
+            nc.scalar.activation(pag[:], pa[:], ACT.Copy, scale=gs_t[:, t:t + 1])
+            nc.scalar.activation(root[:], size[:], ACT.Abs_reciprocal_sqrt, bias=0.5)
+            nc.scalar.activation(inv[:], root[:], ACT.Square)
+            z_win[t] = keep.tile([P, S * (2 - t % 2)], F32, name="z_win%d" % t, tag="turn%d" % t if t % 2 == 0 else "odd%d" % t, align_bytes=64)
+            nc.vector.tensor_tensor(big[:], pa[:], pb[:], ALU.max)
+            if t % 2 == 0:
+                nc.scalar.copy(z_win[t][:, S:2 * S], z_win[t + 1][:])
+            nc.vector.tensor_tensor(z_win[t][:].indirect(n2_t[:]), big[:], gs_wide[t][:], ALU.mult)
+            nc.vector.tensor_tensor(z_win[t][:].indirect(n1_t[:]), pag[:], inv[:], ALU.mult)
+
+        z4 = keep.tile([P, S, NT], BF16, name="z4", tag="odd3", align_bytes=64)
+        nc.scalar.copy(z4[:, :, 0:2], z_win[0][:].rearrange("p (u j) -> p j u", u=2))
+        zw = sb("zw", [P, S], U32)
+        zs = sb("zs", [P, S], U8)
+        for c in range(2):
+            cols = slice(W * c, W * (c + 1))
+            nc.vector.tensor_copy(z4[:, cols, 2:4], z_win[2][:].rearrange("p (u j) -> p j u", u=2)[:, cols, :])
+            nc.vector.quantize_mx(
+                out=zw[:, cols].bitcast(FP8X4), scales=zs[:, cols],
+                in_=z4[:, cols, :].rearrange("p j t -> p (j t)"),
+            )
+
+        halves = [slice(0, W), slice(W, S)]
+        first = [psum.tile([P, W], F32, name="h_first%d" % c, tag="bank%d" % (4 + c)) for c in range(2)]
+        rest = [psum.tile([P, S], F32, name="h_bank%d" % t, tag="bank%d" % ((5 + t) % 8)) for t in range(1, NT)]
+        for c, cols in enumerate(halves):
+            for t in range(NT):
+                rows = slice(P * t, P * (t + 1))
+                nc.tensor.matmul_mx(
+                    out=first[c][:] if t == 0 else rest[t - 1][:, cols],
+                    lhsT=dw[:, rows].bitcast(FP8X4), lhsT_scale=ds_plane[:, rows],
+                    rhs=zw[:, cols].bitcast(FP8X4), rhs_scale=zs[:, cols], start=True, stop=True,
+                )
+        h = [sb("h%d" % t, [P, S], F32) for t in range(NT)]
+        for c, cols in enumerate(halves):
+            nc.scalar.activation(h[0][:, cols], first[c][:], ACT.Copy, scale=0.0625)
+        for t in range(1, NT):
+            nc.scalar.activation(h[t][:], rest[t - 1][:], ACT.Copy, scale=0.0625)
+
+        out_rows = out.rearrange("(p t) n -> p t n", t=NT)
+
+        def entries(cols):
+            return slice(cols.start // 16, cols.stop // 16)
+
+        for t in range(NT):
+            sent = keep.tile([P, 2 * S], F32, name="sent%d" % t, tag="sent%d" % t if t < 2 else "back%d_0" % (t - 2), align_bytes=64)
+            for cols in halves if t == 0 else [slice(0, S)]:
+                nc.vector.tensor_copy(sent[:].indirect(n3_t[:, entries(cols)]), h[t][:, cols])
+            for c, cols in enumerate(halves if t == NT - 1 else [slice(0, S)]):
+                width = cols.stop - cols.start
+                back = keep.tile([P, width], F32, name="back%d_%d" % (t, c), tag="back%d_%d" % (t, c), align_bytes=64)
+                res = sb("res%d_%d" % (t, c), [P, width], F32)
+                nc.scalar.activation(back[:], sent[:].indirect(n4_t[:, entries(cols)]), ACT.Copy)
+                nc.vector.tensor_tensor(res[:], back[:], h[t][:, cols], ALU.max)
+                nc.sync.dma_start(out_rows[:, t, cols], res[:])

@@ -16,6 +16,7 @@ ALU = mybir.AluOpType
 P = 128
 K, T, S, H, W, G = 512, 1024, 512, 512, 256, 2048
 NT = 4
+SPLIT = 320
 FLOPS = 3 * 2 * K * H * S
 
 
@@ -62,6 +63,11 @@ def tile_picked_thqratiorelay_none_p_kernel(
         nc.gpsimd.dma_start(ww_raw[0][:].bitcast(I32), w1_words[0].bitcast(I32))
         nc.gpsimd.dma_start(ww_raw[1][:].bitcast(I32), w2_words[0].bitcast(I32))
 
+        warm_in = sb("warm_in", [P, 1], F32)
+        warm_out = sb("warm_out", [P, 1], F32)
+        nc.vector.memset(warm_in[:], 1.0)
+        nc.scalar.activation(warm_out[:], warm_in[:], ACT.Abs_reciprocal_sqrt, bias=0.5)
+
         ds_tab = sb("ds_tab", [P, G], U8)
         gs_t = sb("gs_t", [P, NT], F32)
         nc.gpsimd.dma_start(ds_tab[:].bitcast(I32), spread_rows(d_scales))
@@ -90,111 +96,174 @@ def tile_picked_thqratiorelay_none_p_kernel(
                 ww[i][:].bitcast(U16).rearrange("p (t m) -> p t m", t=NT),
                 ww_raw[i][:].bitcast(U16).rearrange("p (m t) -> p t m", t=NT),
             )
-        gs_wide = [sb("gs_wide%d" % t, [P, W], F32) for t in range(NT)]
-        for t in range(NT):
+        gs_wide = {t: sb("gs_wide%d" % t, [P, W], F32) for t in (0, 2)}
+        for t in (0, 2):
             nc.scalar.copy(gs_wide[t][:], gs_t[:, t:t + 1].to_broadcast([P, W]))
 
         xs_got = sb("xs_got", [P, 2 * S], U8)
         nc.vector.tensor_copy(xs_got[:, S:2 * S], xs_tab[:].indirect(hz_t[:]))
         nc.vector.tensor_copy(xs_got[:, 0:S], xs_tab[:].indirect(offs_t[:]))
         place_rows(nc.sync, xs_plane, xs_got)
-        xw_got = [sb("xw_got%d" % i, [P, S], U32) for i in range(2)]
-        nc.vector.tensor_copy(xw_got[0][:], xw_tab[:].bitcast(U32).indirect(offs_t[:]))
-        nc.vector.tensor_copy(xw_got[1][:], xw_tab[:].bitcast(U32).indirect(hz_t[:]))
+        halves = [slice(0, W), slice(W, S)]
 
-        y_bank = [psum.tile([P, S], F32, name="y_bank%d" % t, tag="bank%d" % t) for t in range(NT)]
-        for t in (1, 3, 0, 2):
-            for i in range(2):
-                nc.tensor.matmul_mx(
-                    out=y_bank[t][:],
-                    lhsT=ww[i][:, 2 * P * t:2 * P * (t + 1)].bitcast(FP4X4),
-                    lhsT_scale=ws_plane[:, H * i + P * t:H * i + P * (t + 1)],
-                    rhs=xw_got[i][:].bitcast(FP8X4),
-                    rhs_scale=xs_plane[:, S * i:S * (i + 1)],
-                    start=(i == 0),
-                    stop=(i == 1),
-                )
+        def entries(cols):
+            return slice(cols.start // 16, cols.stop // 16)
+
+        def bank(number, width):
+            return psum.tile([P, width], F32, name="bank%d" % number, tag="bank%d" % number)
+
+        xw_got = [sb("xw_got%d" % i, [P, S], U32) for i in range(2)]
+        for cols in halves:
+            for i, picks in enumerate((offs_t, hz_t)):
+                nc.vector.tensor_copy(xw_got[i][:, cols], xw_tab[:].bitcast(U32).indirect(picks[:, entries(cols)]))
+
+        order = (1, 3, 0, 2)
+        y_parts = {}
+        number = 0
+        for t in order:
+            y_parts[t] = []
+            for cols in halves if t == order[0] else [slice(0, S)]:
+                acc = bank(number, cols.stop - cols.start)
+                number = number + 1
+                y_parts[t].append((cols, acc))
+                for i in range(2):
+                    nc.tensor.matmul_mx(
+                        out=acc[:],
+                        lhsT=ww[i][:, 2 * P * t:2 * P * (t + 1)].bitcast(FP4X4),
+                        lhsT_scale=ws_plane[:, H * i + P * t:H * i + P * (t + 1)],
+                        rhs=xw_got[i][:, cols].bitcast(FP8X4),
+                        rhs_scale=xs_plane[:, S * i + cols.start:S * i + cols.stop],
+                        start=(i == 0),
+                        stop=(i == 1),
+                    )
 
         ds_got = sb("ds_got", [P, H], U8)
         nc.vector.tensor_copy(ds_got[:], ds_tab[:].indirect(k1_t[:]))
         ds_dealt = sb("ds_dealt", [P, H], U8)
         nc.vector.tensor_copy(
-            ds_dealt[:].rearrange("p (t m) -> p t m", t=NT), ds_got[:].rearrange("p (m t) -> p t m", t=NT)
+            ds_dealt[:].bitcast(I32).rearrange("p (t r w) -> p t r w", t=NT, r=8),
+            ds_got[:].bitcast(I32).rearrange("p (r t w) -> p t r w", t=NT, r=8),
         )
-        place_rows(nc.gpsimd, ds_plane, ds_dealt)
+        place_rows(nc.sync, ds_plane, ds_dealt)
         dw_got = sb("dw_got", [P, H], U32)
         nc.vector.tensor_copy(dw_got[:], dw_tab[:].bitcast(U32).indirect(k1_t[:]))
-        dw = sb("dw", [P, H], U32)
-        nc.vector.tensor_copy(
-            dw[:].rearrange("p (t m) -> p t m", t=NT), dw_got[:].rearrange("p (m t) -> p t m", t=NT)
-        )
-
-        z_win = {}
-        for t in (1, 3, 0, 2):
-            y = sb("y%d" % t, [P, S], F32)
-            nc.scalar.copy(y[:], y_bank[t][:])
-            pa = sb("pa%d" % t, [P, W], F32)
-            pb = sb("pb%d" % t, [P, W], F32)
-            nc.scalar.activation(pb[:], y[:].indirect(n2_t[:]), ACT.Copy)
-            nc.scalar.activation(pa[:], y[:].indirect(n1_t[:]), ACT.Copy)
-            size = sb("size%d" % t, [P, W], F32)
-            root = keep.tile([P, W], F32, name="root%d" % t, tag="turn%d" % t, align_bytes=64)
-            inv = sb("inv%d" % t, [P, W], F32)
-            pag = sb("pag%d" % t, [P, W], F32)
-            big = sb("big%d" % t, [P, W], F32)
-            nc.scalar.activation(size[:], pb[:], ACT.Abs)
-            nc.scalar.activation(pag[:], pa[:], ACT.Copy, scale=gs_t[:, t:t + 1])
-            nc.scalar.activation(root[:], size[:], ACT.Abs_reciprocal_sqrt, bias=0.5)
-            nc.scalar.activation(inv[:], root[:], ACT.Square)
-            z_win[t] = keep.tile([P, S * (2 - t % 2)], F32, name="z_win%d" % t, tag="turn%d" % t if t % 2 == 0 else "odd%d" % t, align_bytes=64)
-            nc.vector.tensor_tensor(big[:], pa[:], pb[:], ALU.max)
-            if t % 2 == 0:
-                nc.scalar.copy(z_win[t][:, S:2 * S], z_win[t + 1][:])
-            nc.vector.tensor_tensor(z_win[t][:].indirect(n2_t[:]), big[:], gs_wide[t][:], ALU.mult)
-            nc.vector.tensor_tensor(z_win[t][:].indirect(n1_t[:]), pag[:], inv[:], ALU.mult)
-
-        z4 = keep.tile([P, S, NT], BF16, name="z4", tag="odd3", align_bytes=64)
-        nc.scalar.copy(z4[:, :, 0:2], z_win[0][:].rearrange("p (u j) -> p j u", u=2))
-        zw = sb("zw", [P, S], U32)
-        zs = sb("zs", [P, S], U8)
-        for c in range(2):
-            cols = slice(W * c, W * (c + 1))
-            nc.vector.tensor_copy(z4[:, cols, 2:4], z_win[2][:].rearrange("p (u j) -> p j u", u=2)[:, cols, :])
-            nc.vector.quantize_mx(
-                out=zw[:, cols].bitcast(FP8X4), scales=zs[:, cols],
-                in_=z4[:, cols, :].rearrange("p j t -> p (j t)"),
+        dw = [sb("dw%d" % t, [P, P], U32) for t in range(NT)]
+        for t in range(NT):
+            nc.sync.dma_start(
+                dw[t][:].bitcast(I32).rearrange("p (r q) -> p r q", r=8),
+                dw_got[:].bitcast(I32).rearrange("p (r t q) -> p t r q", t=NT, r=8)[:, t],
             )
 
-        halves = [slice(0, W), slice(W, S)]
-        first = [psum.tile([P, W], F32, name="h_first%d" % c, tag="bank%d" % (4 + c)) for c in range(2)]
-        rest = [psum.tile([P, S], F32, name="h_bank%d" % t, tag="bank%d" % ((5 + t) % 8)) for t in range(1, NT)]
-        for c, cols in enumerate(halves):
-            for t in range(NT):
-                rows = slice(P * t, P * (t + 1))
-                nc.tensor.matmul_mx(
-                    out=first[c][:] if t == 0 else rest[t - 1][:, cols],
-                    lhsT=dw[:, rows].bitcast(FP8X4), lhsT_scale=ds_plane[:, rows],
-                    rhs=zw[:, cols].bitcast(FP8X4), rhs_scale=zs[:, cols], start=True, stop=True,
-                )
+        z_win = {}
+        pa, pb = {}, {}
+
+        def shared(name, shape, dtype, tag):
+            return keep.tile(shape, dtype, name=name, tag=tag, align_bytes=64)
+
+        big = {}
+
+        def fetch(t):
+            y = shared("y%d" % t, [P, S], F32, "y")
+            for cols, acc in y_parts[t]:
+                nc.scalar.copy(y[:, cols], acc[:])
+            pa[t] = sb("pa%d" % t, [P, W], F32)
+            pb[t] = sb("pb%d" % t, [P, W], F32)
+            nc.scalar.activation(pb[t][:], y[:].indirect(n2_t[:]), ACT.Copy)
+            nc.scalar.activation(pa[t][:], y[:].indirect(n1_t[:]), ACT.Copy)
+            big[t] = sb("big%d" % t, [P, W], F32)
+            nc.vector.tensor_tensor(big[t][:], pa[t][:], pb[t][:], ALU.max)
+
+        def put_larger(t, before):
+            if t % 2 == 0:
+                z_win[t] = shared("z_win%d" % t, [P, 2 * S], F32, "root%d" % before)
+                nc.scalar.activation(z_win[t][:, S:2 * S], z_win[t + 1][:], ACT.Copy, scale=gs_t[:, t + 1:t + 2])
+                nc.vector.tensor_tensor(z_win[t][:].indirect(n2_t[:]), big[t][:], gs_wide[t][:], ALU.mult)
+            else:
+                z_win[t] = sb("z_win%d" % t, [P, S], F32)
+                nc.vector.tensor_copy(z_win[t][:].indirect(n2_t[:]), big[t][:])
+
+        def put_ratio(t):
+            size = sb("size%d" % t, [P, W], F32)
+            root = shared("root%d" % t, [P, W], F32, "root%d" % t)
+            inv = sb("inv%d" % t, [P, W], F32)
+            nc.scalar.activation(size[:], pb[t][:], ACT.Abs)
+            top = pa[t]
+            if t % 2 == 0:
+                top = sb("top%d" % t, [P, W], F32)
+                nc.scalar.activation(top[:], pa[t][:], ACT.Copy, scale=gs_t[:, t:t + 1])
+            nc.scalar.activation(root[:], size[:], ACT.Abs_reciprocal_sqrt, bias=0.5)
+            nc.scalar.activation(inv[:], root[:], ACT.Square)
+            nc.vector.tensor_tensor(z_win[t][:].indirect(n1_t[:]), top[:], inv[:], ALU.mult)
+
+        fetch(order[0])
+        put_larger(order[0], None)
+        for before, t in zip(order, order[1:]):
+            fetch(t)
+            put_ratio(before)
+            put_larger(t, before)
+        put_ratio(order[-1])
+
+        lead, rest = slice(0, P), slice(P, S)
+        z4 = {
+            0: sb("z4_lead", [P, P, NT], BF16),
+            P: shared("z4_rest", [P, S - P, NT], BF16, "root%d" % order[-1]),
+        }
+        pairs = [z_win[t][:].rearrange("p (u j) -> p j u", u=2) for t in (0, 2)]
+        for cols in (rest, lead):
+            nc.scalar.copy(z4[cols.start][:, :, 0:2], pairs[0][:, cols, :])
+        nc.vector.tensor_copy(z4[0][:, :, 2:4], pairs[1][:, lead, :])
+        nc.vector.tensor_copy(z4[P][:, 0:SPLIT - P, 2:4], pairs[1][:, P:SPLIT, :])
+        nc.scalar.copy(z4[P][:, SPLIT - P:S - P, 2:4], pairs[1][:, SPLIT:S, :])
+        zw = sb("zw", [P, S], U32)
+        zs = sb("zs", [P, S], U8)
+        for cols in (lead, rest):
+            nc.vector.quantize_mx(
+                out=zw[:, cols].bitcast(FP8X4), scales=zs[:, cols],
+                in_=z4[cols.start][:].rearrange("p j t -> p (j t)"),
+            )
+
+        def second_product(acc, t, cols):
+            nc.tensor.matmul_mx(
+                out=acc, lhsT=dw[t][:].bitcast(FP8X4), lhsT_scale=ds_plane[:, P * t:P * (t + 1)],
+                rhs=zw[:, cols].bitcast(FP8X4), rhs_scale=zs[:, cols], start=True, stop=True,
+            )
+
         h = [sb("h%d" % t, [P, S], F32) for t in range(NT)]
-        for c, cols in enumerate(halves):
-            nc.scalar.activation(h[0][:, cols], first[c][:], ACT.Copy, scale=0.0625)
-        for t in range(1, NT):
-            nc.scalar.activation(h[t][:], rest[t - 1][:], ACT.Copy, scale=0.0625)
+        for t in range(2):
+            acc = bank(5 + t, P)
+            second_product(acc[:], t, lead)
+            nc.scalar.activation(h[t][:, lead], acc[:], ACT.Copy, scale=0.0625)
+        for t in range(2):
+            acc = bank((7 + t) % 8, S - P)
+            second_product(acc[:, 0:P], t, slice(P, W))
+            second_product(acc[:, P:S - P], t, slice(W, S))
+            nc.scalar.activation(h[t][:, rest], acc[:], ACT.Copy, scale=0.0625)
+        for t in range(2, NT):
+            acc = bank(t - 1, S)
+            second_product(acc[:], t, slice(0, S))
+            nc.scalar.activation(h[t][:], acc[:], ACT.Copy, scale=0.0625)
 
-        out_rows = out.rearrange("(p t) n -> p t n", t=NT)
+        out_rows = out.rearrange("(r t q) n -> t r q n", t=NT, r=8)
+        sent = {}
 
-        def entries(cols):
-            return slice(cols.start // 16, cols.stop // 16)
+        def send(t, cols):
+            if cols.start == 0:
+                sent[t] = shared("sent%d" % t, [P, 2 * S], F32, "sent%d" % (t % 2))
+            nc.vector.tensor_copy(sent[t][:].indirect(n3_t[:, entries(cols)]), h[t][:, cols])
 
-        for t in range(NT):
-            sent = keep.tile([P, 2 * S], F32, name="sent%d" % t, tag="sent%d" % t if t < 2 else "back%d_0" % (t - 2), align_bytes=64)
-            for cols in halves if t == 0 else [slice(0, S)]:
-                nc.vector.tensor_copy(sent[:].indirect(n3_t[:, entries(cols)]), h[t][:, cols])
+        def finish(t):
             for c, cols in enumerate(halves if t == NT - 1 else [slice(0, S)]):
                 width = cols.stop - cols.start
-                back = keep.tile([P, width], F32, name="back%d_%d" % (t, c), tag="back%d_%d" % (t, c), align_bytes=64)
+                back = sb("back%d_%d" % (t, c), [P, width], F32)
                 res = sb("res%d_%d" % (t, c), [P, width], F32)
-                nc.scalar.activation(back[:], sent[:].indirect(n4_t[:, entries(cols)]), ACT.Copy)
+                nc.scalar.activation(back[:], sent[t][:].indirect(n4_t[:, entries(cols)]), ACT.Copy)
                 nc.vector.tensor_tensor(res[:], back[:], h[t][:, cols], ALU.max)
-                nc.sync.dma_start(out_rows[:, t, cols], res[:])
+                nc.sync.dma_start(out_rows[t][:, :, cols], res[:])
+
+        for cols in (lead, rest):
+            for t in range(2):
+                send(t, cols)
+        for t in range(NT):
+            finish(t)
+            if t + 2 < NT:
+                send(t + 2, slice(0, S))

from contextlib import ExitStack

import concourse.mybir as mybir

F32 = mybir.dt.float32
BF16 = mybir.dt.bfloat16
I32 = mybir.dt.int32
U32 = mybir.dt.uint32
U16 = mybir.dt.uint16
U8 = mybir.dt.uint8
FP8X4 = mybir.dt.float8_e4m3fn_x4
FP4X4 = mybir.dt.float4_e2m1fn_x4
ACT = mybir.ActivationFunctionType
ALU = mybir.AluOpType

P = 128
K, T, S, H, W, G = 512, 1024, 512, 512, 256, 2048
NT = 4
SPLIT = 320
FLOPS = 3 * 2 * K * H * S


def tile_picked_thqratiorelay_none_p_kernel(
    tc, x_words, x_scales, w1_words, w1_scales, w2_words, w2_scales, gs, d_words, d_scales,
    offs, hz, n1, n2, k1, n3, n4, out,
):
    nc = tc.nc
    with ExitStack() as ctx:
        keep = ctx.enter_context(tc.tile_pool(name="keep", bufs=1))
        psum = ctx.enter_context(tc.psum_pool(name="psum", bufs=1))

        def sb(name, shape, dtype):
            return keep.tile(shape, dtype, name=name, align_bytes=64)

        def zeroed_bytes(name, width):
            tile = sb(name, [P, width], U8)
            nc.vector.memset(tile[:].bitcast(I32), 0)
            return tile

        def load_list(name, src):
            tile = sb(name, list(src.shape), U16)
            nc.sync.dma_start(tile[:], src)
            return tile

        def spread_rows(scales):
            rows = scales[0].bitcast(I32)
            return rows.unsqueeze(1).to_broadcast([16, 8, rows.shape[1]])

        def place_rows(queue, plane, spread):
            for j in range(4):
                queue.dma_start(plane[j:P:32, :].bitcast(I32), spread[8 * j:P:32, :].bitcast(I32))

        xs_tab = sb("xs_tab", [P, T], U8)
        ws_raw = sb("ws_raw", [P, 2 * H], U8)
        ww_raw = [sb("ww_raw%d" % i, [P, 2 * H], U8) for i in range(2)]
        xw_tab = sb("xw_tab", [P, T], I32)
        nc.scalar.dma_start(xs_tab[:].bitcast(I32), spread_rows(x_scales))
        hz_t = load_list("hz_t", hz)
        offs_t = load_list("offs_t", offs)
        nc.scalar.dma_start(ws_raw[:, 0:H].bitcast(I32), spread_rows(w1_scales))
        nc.scalar.dma_start(ws_raw[:, H:2 * H].bitcast(I32), spread_rows(w2_scales))
        nc.sync.dma_start(xw_tab[:], x_words[0].rearrange("p n r -> p (n r)").bitcast(I32))
        nc.gpsimd.dma_start(ww_raw[0][:].bitcast(I32), w1_words[0].bitcast(I32))
        nc.gpsimd.dma_start(ww_raw[1][:].bitcast(I32), w2_words[0].bitcast(I32))

        warm_in = sb("warm_in", [P, 1], F32)
        warm_out = sb("warm_out", [P, 1], F32)
        nc.vector.memset(warm_in[:], 1.0)
        nc.scalar.activation(warm_out[:], warm_in[:], ACT.Abs_reciprocal_sqrt, bias=0.5)

        ds_tab = sb("ds_tab", [P, G], U8)
        gs_t = sb("gs_t", [P, NT], F32)
        nc.gpsimd.dma_start(ds_tab[:].bitcast(I32), spread_rows(d_scales))
        nc.gpsimd.dma_start(gs_t[:], gs.rearrange("(p t) o -> p (t o)", t=NT))
        k1_t = load_list("k1_t", k1)
        dw_tab = sb("dw_tab", [P, G], I32)
        nc.sync.dma_start(dw_tab[:], d_words[0].rearrange("p n r -> p (n r)").bitcast(I32))
        n2_t = load_list("n2_t", n2)
        n1_t = load_list("n1_t", n1)
        n3_t = load_list("n3_t", n3)
        n4_t = load_list("n4_t", n4)

        ws_plane = zeroed_bytes("ws_plane", 2 * H)
        xs_plane = zeroed_bytes("xs_plane", 2 * S)
        ds_plane = zeroed_bytes("ds_plane", H)

        ws_dealt = sb("ws_dealt", [P, 2 * H], U8)
        nc.vector.tensor_copy(
            ws_dealt[:].rearrange("p (i t m) -> p i t m", i=2, t=NT),
            ws_raw[:].rearrange("p (i m t) -> p i t m", i=2, t=NT),
        )
        place_rows(nc.sync, ws_plane, ws_dealt)
        ww = [sb("ww%d" % i, [P, 2 * H], U8) for i in range(2)]
        for i in range(2):
            nc.scalar.copy(
                ww[i][:].bitcast(U16).rearrange("p (t m) -> p t m", t=NT),
                ww_raw[i][:].bitcast(U16).rearrange("p (m t) -> p t m", t=NT),
            )
        gs_wide = {t: sb("gs_wide%d" % t, [P, W], F32) for t in (0, 2)}
        for t in (0, 2):
            nc.scalar.copy(gs_wide[t][:], gs_t[:, t:t + 1].to_broadcast([P, W]))

        xs_got = sb("xs_got", [P, 2 * S], U8)
        nc.vector.tensor_copy(xs_got[:, S:2 * S], xs_tab[:].indirect(hz_t[:]))
        nc.vector.tensor_copy(xs_got[:, 0:S], xs_tab[:].indirect(offs_t[:]))
        place_rows(nc.sync, xs_plane, xs_got)
        halves = [slice(0, W), slice(W, S)]

        def entries(cols):
            return slice(cols.start // 16, cols.stop // 16)

        def bank(number, width):
            return psum.tile([P, width], F32, name="bank%d" % number, tag="bank%d" % number)

        xw_got = [sb("xw_got%d" % i, [P, S], U32) for i in range(2)]
        for cols in halves:
            for i, picks in enumerate((offs_t, hz_t)):
                nc.vector.tensor_copy(xw_got[i][:, cols], xw_tab[:].bitcast(U32).indirect(picks[:, entries(cols)]))

        order = (1, 3, 0, 2)
        y_parts = {}
        number = 0
        for t in order:
            y_parts[t] = []
            for cols in halves if t == order[0] else [slice(0, S)]:
                acc = bank(number, cols.stop - cols.start)
                number = number + 1
                y_parts[t].append((cols, acc))
                for i in range(2):
                    nc.tensor.matmul_mx(
                        out=acc[:],
                        lhsT=ww[i][:, 2 * P * t:2 * P * (t + 1)].bitcast(FP4X4),
                        lhsT_scale=ws_plane[:, H * i + P * t:H * i + P * (t + 1)],
                        rhs=xw_got[i][:, cols].bitcast(FP8X4),
                        rhs_scale=xs_plane[:, S * i + cols.start:S * i + cols.stop],
                        start=(i == 0),
                        stop=(i == 1),
                    )

        ds_got = sb("ds_got", [P, H], U8)
        nc.vector.tensor_copy(ds_got[:], ds_tab[:].indirect(k1_t[:]))
        ds_dealt = sb("ds_dealt", [P, H], U8)
        nc.vector.tensor_copy(
            ds_dealt[:].bitcast(I32).rearrange("p (t r w) -> p t r w", t=NT, r=8),
            ds_got[:].bitcast(I32).rearrange("p (r t w) -> p t r w", t=NT, r=8),
        )
        place_rows(nc.sync, ds_plane, ds_dealt)
        dw_got = sb("dw_got", [P, H], U32)
        nc.vector.tensor_copy(dw_got[:], dw_tab[:].bitcast(U32).indirect(k1_t[:]))
        dw = [sb("dw%d" % t, [P, P], U32) for t in range(NT)]
        for t in range(NT):
            nc.sync.dma_start(
                dw[t][:].bitcast(I32).rearrange("p (r q) -> p r q", r=8),
                dw_got[:].bitcast(I32).rearrange("p (r t q) -> p t r q", t=NT, r=8)[:, t],
            )

        z_win = {}
        pa, pb = {}, {}

        def shared(name, shape, dtype, tag):
            return keep.tile(shape, dtype, name=name, tag=tag, align_bytes=64)

        big = {}

        def fetch(t):
            y = shared("y%d" % t, [P, S], F32, "y")
            for cols, acc in y_parts[t]:
                nc.scalar.copy(y[:, cols], acc[:])
            pa[t] = sb("pa%d" % t, [P, W], F32)
            pb[t] = sb("pb%d" % t, [P, W], F32)
            nc.scalar.activation(pb[t][:], y[:].indirect(n2_t[:]), ACT.Copy)
            nc.scalar.activation(pa[t][:], y[:].indirect(n1_t[:]), ACT.Copy)
            big[t] = sb("big%d" % t, [P, W], F32)
            nc.vector.tensor_tensor(big[t][:], pa[t][:], pb[t][:], ALU.max)

        def put_larger(t, before):
            if t % 2 == 0:
                z_win[t] = shared("z_win%d" % t, [P, 2 * S], F32, "root%d" % before)
                nc.scalar.activation(z_win[t][:, S:2 * S], z_win[t + 1][:], ACT.Copy, scale=gs_t[:, t + 1:t + 2])
                nc.vector.tensor_tensor(z_win[t][:].indirect(n2_t[:]), big[t][:], gs_wide[t][:], ALU.mult)
            else:
                z_win[t] = sb("z_win%d" % t, [P, S], F32)
                nc.vector.tensor_copy(z_win[t][:].indirect(n2_t[:]), big[t][:])

        def put_ratio(t):
            size = sb("size%d" % t, [P, W], F32)
            root = shared("root%d" % t, [P, W], F32, "root%d" % t)
            inv = sb("inv%d" % t, [P, W], F32)
            nc.scalar.activation(size[:], pb[t][:], ACT.Abs)
            top = pa[t]
            if t % 2 == 0:
                top = sb("top%d" % t, [P, W], F32)
                nc.scalar.activation(top[:], pa[t][:], ACT.Copy, scale=gs_t[:, t:t + 1])
            nc.scalar.activation(root[:], size[:], ACT.Abs_reciprocal_sqrt, bias=0.5)
            nc.scalar.activation(inv[:], root[:], ACT.Square)
            nc.vector.tensor_tensor(z_win[t][:].indirect(n1_t[:]), top[:], inv[:], ALU.mult)

        fetch(order[0])
        put_larger(order[0], None)
        for before, t in zip(order, order[1:]):
            fetch(t)
            put_ratio(before)
            put_larger(t, before)
        put_ratio(order[-1])

        lead, rest = slice(0, P), slice(P, S)
        z4 = {
            0: sb("z4_lead", [P, P, NT], BF16),
            P: shared("z4_rest", [P, S - P, NT], BF16, "root%d" % order[-1]),
        }
        pairs = [z_win[t][:].rearrange("p (u j) -> p j u", u=2) for t in (0, 2)]
        for cols in (rest, lead):
            nc.scalar.copy(z4[cols.start][:, :, 0:2], pairs[0][:, cols, :])
        nc.vector.tensor_copy(z4[0][:, :, 2:4], pairs[1][:, lead, :])
        nc.vector.tensor_copy(z4[P][:, 0:SPLIT - P, 2:4], pairs[1][:, P:SPLIT, :])
        nc.scalar.copy(z4[P][:, SPLIT - P:S - P, 2:4], pairs[1][:, SPLIT:S, :])
        zw = sb("zw", [P, S], U32)
        zs = sb("zs", [P, S], U8)
        for cols in (lead, rest):
            nc.vector.quantize_mx(
                out=zw[:, cols].bitcast(FP8X4), scales=zs[:, cols],
                in_=z4[cols.start][:].rearrange("p j t -> p (j t)"),
            )

        def second_product(acc, t, cols):
            nc.tensor.matmul_mx(
                out=acc, lhsT=dw[t][:].bitcast(FP8X4), lhsT_scale=ds_plane[:, P * t:P * (t + 1)],
                rhs=zw[:, cols].bitcast(FP8X4), rhs_scale=zs[:, cols], start=True, stop=True,
            )

        h = [sb("h%d" % t, [P, S], F32) for t in range(NT)]
        for t in range(2):
            acc = bank(5 + t, P)
            second_product(acc[:], t, lead)
            nc.scalar.activation(h[t][:, lead], acc[:], ACT.Copy, scale=0.0625)
        for t in range(2):
            acc = bank((7 + t) % 8, S - P)
            second_product(acc[:, 0:P], t, slice(P, W))
            second_product(acc[:, P:S - P], t, slice(W, S))
            nc.scalar.activation(h[t][:, rest], acc[:], ACT.Copy, scale=0.0625)
        for t in range(2, NT):
            acc = bank(t - 1, S)
            second_product(acc[:], t, slice(0, S))
            nc.scalar.activation(h[t][:], acc[:], ACT.Copy, scale=0.0625)

        out_rows = out.rearrange("(r t q) n -> t r q n", t=NT, r=8)
        sent = {}

        def send(t, cols):
            if cols.start == 0:
                sent[t] = shared("sent%d" % t, [P, 2 * S], F32, "sent%d" % (t % 2))
            nc.vector.tensor_copy(sent[t][:].indirect(n3_t[:, entries(cols)]), h[t][:, cols])

        def finish(t):
            for c, cols in enumerate(halves if t == NT - 1 else [slice(0, S)]):
                width = cols.stop - cols.start
                back = sb("back%d_%d" % (t, c), [P, width], F32)
                res = sb("res%d_%d" % (t, c), [P, width], F32)
                nc.scalar.activation(back[:], sent[t][:].indirect(n4_t[:, entries(cols)]), ACT.Copy)
                nc.vector.tensor_tensor(res[:], back[:], h[t][:, cols], ALU.max)
                nc.sync.dma_start(out_rows[t][:, :, cols], res[:])

        for cols in (lead, rest):
            for t in range(2):
                send(t, cols)
        for t in range(NT):
            finish(t)
            if t + 2 < NT:
                send(t + 2, slice(0, S))
